import numpy as np
import ml_dtypes


def mxq(x, axis, fmt="e4m3"):
    dtype, down = {"e4m3": (ml_dtypes.float8_e4m3fn, 7), "e5m2": (ml_dtypes.float8_e5m2, 14)}[fmt]
    v = np.moveaxis(np.asarray(x, np.float32).astype(ml_dtypes.bfloat16).astype(np.float64), axis, -1)
    blocks = v.reshape(v.shape[:-1] + (-1, 32))
    amax = np.abs(blocks).max(-1, keepdims=True)
    byte = np.maximum(np.where(amax > 0, np.frexp(amax)[1] - 1 + 127, 0) - down, 1)
    scale = np.exp2(byte - 127.0)
    codes = (blocks / scale).astype(np.float32).astype(dtype).astype(np.float64)
    return np.moveaxis((codes * scale).reshape(v.shape), -1, axis)


WIDE = False


def mx_kscale(k):
    if not WIDE:
        return np.ones(k)
    levels = np.array([10, -10, 5, -5, 0])
    if k % 512:
        return np.exp2(np.random.permutation(np.resize(levels, k // 32))).repeat(32)
    a = np.empty((k // 512, 16))
    for p in range(k // 512):
        a[p, :8] = np.random.permutation(np.resize(levels, 8))
        for g in range(8):
            far = levels[np.abs(levels - a[p, g]) >= 10]
            a[p, g + 8] = far[np.random.randint(len(far))]
    return np.exp2(a.ravel()).repeat(32)


def f64(x):
    return np.asarray(x).astype(np.float64)


def striped8(idx):
    return np.asarray(idx).reshape(8, -1, 16).transpose(0, 2, 1).reshape(128, -1).astype(np.uint16)


def unstriped8(offs):
    return offs.reshape(8, 16, -1).transpose(0, 2, 1).reshape(8, -1).astype(np.int64)


def pick8(x, idx, run):
    r = np.arange(len(x))
    return x[r[:, None], idx[r % (8 * run) // run]]


E2M1 = np.array([0.0, 0.5, 1.0, 1.5, 2.0, 3.0, 4.0, 6.0, -0.0, -0.5, -1.0, -1.5, -2.0, -3.0, -4.0, -6.0])


def pack_weight(w, fmt):
    k, n = w.shape
    w = f64(np.asarray(w, np.float32).astype(ml_dtypes.bfloat16)).reshape(k // 32, 32, n)
    amax = np.abs(w).max(1)
    if fmt == "e4m3":
        byte = np.frexp(amax)[1] - 1 + 127 - 7
    else:
        mant, ex = np.frexp(amax / 6.0)
        byte = np.where(mant > 0.5, ex, ex - 1) + 127
    byte = np.clip(np.where(amax > 0, byte, 1), 1, 254)
    scaled = (w * np.exp2(127.0 - byte)[:, None, :]).reshape(k, n).astype(np.float32)
    by_word = np.ascontiguousarray(scaled.reshape(k // 512, 128, 4, n).transpose(0, 1, 3, 2))
    if fmt == "e4m3":
        words = by_word.astype(ml_dtypes.float8_e4m3fn).view(np.uint8)
    else:
        c = by_word.astype(ml_dtypes.float4_e2m1fn).view(np.uint8) & 0xF
        words = (c[..., 0::2] | (c[..., 1::2] << 4)).reshape(k // 512, 128, 2 * n)
    return np.ascontiguousarray(words), np.ascontiguousarray(byte.astype(np.uint8).reshape(k // 512, 16, n))


def unpack_weight(words, scales, fmt):
    g, _, n = scales.shape
    words = np.ascontiguousarray(words).reshape(g, 128, n, -1)
    if fmt == "e4m3":
        vals = words.view(ml_dtypes.float8_e4m3fn).astype(np.float64)
    else:
        nib = np.empty((g, 128, n, 4), np.uint8)
        nib[..., 0::2] = words & 0xF
        nib[..., 1::2] = words >> 4
        vals = E2M1[nib]
    vals = vals * np.repeat(np.exp2(scales.astype(np.float64) - 127.0), 8, axis=1)[..., None]
    return vals.transpose(0, 1, 3, 2).reshape(g * 512, n)


D, T, U, X, S, I, Q = 512, 1024, 1024, 1024, 1024, 512, 128


def setup_inputs():
    n = np.random.standard_normal
    idx = np.stack([np.random.permutation(T)[:I] for _ in range(8)])
    idx2 = np.stack([np.random.permutation(U)[:I] for _ in range(8)])
    idx3 = np.stack([np.random.permutation(X)[:I] for _ in range(8)])
    idx4 = np.stack([np.random.permutation(S)[:I] for _ in range(8)])
    idx5 = np.stack([np.random.permutation(T)[:I] for _ in range(8)])
    idx6 = np.stack([np.random.permutation(X)[:I] for _ in range(8)])
    fd = mx_kscale(D)
    keysp = pack_weight(n((D, T)) / fd[:, None], "e2m1")
    notesp = pack_weight(n((D, U)) / fd[:, None], "e4m3")
    usersp = pack_weight(n((D, X)) / fd[:, None], "e2m1")
    shelvesp = pack_weight(n((D, S)) / fd[:, None], "e4m3")
    return {
        "query": (n((D, Q)) * 1.0 / np.sqrt(D) * fd[:, None]).astype(np.float32),
        "keys_words": keysp[0],
        "keys_scales": keysp[1],
        "notes_words": notesp[0],
        "notes_scales": notesp[1],
        "users_words": usersp[0],
        "users_scales": usersp[1],
        "shelves_words": shelvesp[0],
        "shelves_scales": shelvesp[1],
        "offs": striped8(idx),
        "offs2": striped8(idx2),
        "offs3": striped8(idx3),
        "offs4": striped8(idx4),
        "offs5": striped8(idx5),
        "offs6": striped8(idx6),
    }


def reference(query, keys_words, keys_scales, notes_words, notes_scales, users_words, users_scales, shelves_words, shelves_scales, offs, offs2, offs3, offs4, offs5, offs6):
    idx = unstriped8(offs)
    idx2 = unstriped8(offs2)
    idx3 = unstriped8(offs3)
    idx4 = unstriped8(offs4)
    idx5 = unstriped8(offs5)
    idx6 = unstriped8(offs6)
    keysu = unpack_weight(keys_words, keys_scales, "e2m1")
    notesu = unpack_weight(notes_words, notes_scales, "e4m3")
    usersu = unpack_weight(users_words, users_scales, "e2m1")
    shelvesu = unpack_weight(shelves_words, shelves_scales, "e4m3")
    queryq = mxq(f64(query), 0, "e4m3")
    a = queryq.T @ keysu
    b = queryq.T @ notesu
    c0 = queryq.T @ usersu
    d0 = queryq.T @ shelvesu
    r = pick8(b, idx2, 16) - pick8(a, idx, 16)
    v = pick8(d0, idx4, 16) - pick8(c0, idx3, 16)
    f1 = np.zeros((Q, T))
    f1[np.arange(Q)[:, None], idx[np.arange(Q) % 128 // 16]] = v
    f2 = np.zeros((Q, X))
    f2[np.arange(Q)[:, None], idx3[np.arange(Q) % 128 // 16]] = r
    aa = a + f1
    cc = c0 + f2
    y = pick8(aa, idx5, 16) - pick8(cc, idx6, 16)
    return y

@@ -1,0 +1,163 @@
+from contextlib import ExitStack
+
+import concourse.mybir as mybir
+
+F32 = mybir.dt.float32
+BF16 = mybir.dt.bfloat16
+I32 = mybir.dt.int32
+U32 = mybir.dt.uint32
+U16 = mybir.dt.uint16
+U8 = mybir.dt.uint8
+FP8X4 = mybir.dt.float8_e4m3fn_x4
+FP4X4 = mybir.dt.float4_e2m1fn_x4
+ADD = mybir.AluOpType.add
+SUBTRACT = mybir.AluOpType.subtract
+COPY = mybir.ActivationFunctionType.Copy
+
+P = 128
+PACK = 4
+ROWS = 128
+COLS = 1024
+BANK = 512
+SLOTS = 512
+FLOPS = 2 * 512 * 128 * 4 * 1024
+
+
+def tile_attend_crossgaps_four_kernel(
+    tc, query, keys_words, keys_scales, notes_words, notes_scales, users_words, users_scales,
+    shelves_words, shelves_scales, offs, offs2, offs3, offs4, offs5, offs6, out,
+):
+    nc = tc.nc
+    with ExitStack() as ctx:
+        keep = ctx.enter_context(tc.tile_pool(name="keep", bufs=1))
+        psum = ctx.enter_context(tc.psum_pool(name="psum", bufs=1))
+
+        names = ("keys", "notes", "users", "shelves")
+        planes = {n: keep.tile([P, COLS], U8, name=n + "_plane", align_bytes=64) for n in names}
+        words = {
+            "keys": keep.tile([P, 2 * COLS], U8, name="keys_codes", align_bytes=64),
+            "notes": keep.tile([P, COLS], U32, name="notes_codes", align_bytes=64),
+            "users": keep.tile([P, 2 * COLS], U8, name="users_codes", align_bytes=64),
+            "shelves": keep.tile([P, COLS], U32, name="shelves_codes", align_bytes=64),
+        }
+        words_hbm = {
+            "keys": keys_words[0],
+            "notes": notes_words[0].rearrange("p n t -> p (n t)"),
+            "users": users_words[0],
+            "shelves": shelves_words[0].rearrange("p n t -> p (n t)"),
+        }
+        scales_hbm = {"keys": keys_scales, "notes": notes_scales, "users": users_scales, "shelves": shelves_scales}
+        f1 = keep.tile([P, COLS], F32, name="f1")
+        f2 = keep.tile([P, COLS], F32, name="f2")
+
+        for n in names:
+            nc.vector.memset(planes[n][:].bitcast(I32), 0)
+        nc.vector.memset(f2[:], 0.0)
+        nc.vector.memset(f1[:], 0.0)
+
+        def load_scales(n):
+            for quad in range(4):
+                nc.sync.dma_start(
+                    planes[n][32 * quad : 32 * quad + 4, :].bitcast(I32),
+                    scales_hbm[n][0, 4 * quad : 4 * quad + 4, :].bitcast(I32),
+                )
+
+        def load_words(n):
+            nc.sync.dma_start(words[n][:].bitcast(I32), words_hbm[n].bitcast(I32))
+
+        def load_list(src, name):
+            t = keep.tile([P, SLOTS // 16], U16, name=name)
+            nc.sync.dma_start(t[:], src)
+            return t
+
+        q_raw = keep.tile([P, PACK, ROWS], F32, name="q_raw")
+        nc.sync.dma_start(q_raw[:], query.rearrange("(p j) w -> p j w", j=PACK))
+        load_scales("keys")
+        load_words("keys")
+        load_words("notes")
+        load_scales("notes")
+        tok = load_list(offs, "tok")
+        load_words("users")
+        note = load_list(offs2, "note")
+        user = load_list(offs3, "user")
+        load_scales("users")
+        load_words("shelves")
+        load_scales("shelves")
+        shelf = load_list(offs4, "shelf")
+        user_out = load_list(offs6, "user_out")
+        tok_out = load_list(offs5, "tok_out")
+
+        q_bf = keep.tile([P, ROWS, PACK], BF16, name="q_bf", align_bytes=64)
+        nc.vector.tensor_copy(
+            q_bf[:].rearrange("p (c i) t -> p c t i", i=4), q_raw[:].rearrange("p t (c i) -> p c t i", i=4)
+        )
+        q_codes = keep.tile([P, ROWS], U32, name="q_codes", align_bytes=64)
+        q_plane = keep.tile([P, ROWS], U8, name="q_plane", align_bytes=64)
+        nc.vector.quantize_mx(
+            out=q_codes[:].bitcast(FP8X4), scales=q_plane[:], in_=q_bf[:].rearrange("p w t -> p (w t)")
+        )
+
+        banks = {}
+
+        def score(n):
+            for h in range(2):
+                bank = psum.tile([P, BANK], F32, name="bank_%s_%d" % (n, h))
+                if n in ("keys", "users"):
+                    rhs = words[n][:, 2 * BANK * h : 2 * BANK * (h + 1)].bitcast(FP4X4)
+                else:
+                    rhs = words[n][:, BANK * h : BANK * (h + 1)].bitcast(FP8X4)
+                nc.tensor.matmul_mx(
+                    out=bank[:], lhsT=q_codes[:].bitcast(FP8X4), lhsT_scale=q_plane[:],
+                    rhs=rhs, rhs_scale=planes[n][:, BANK * h : BANK * (h + 1)], start=True, stop=True,
+                )
+                banks[(n, h)] = bank
+
+        for n in names:
+            score(n)
+
+        a = keep.tile([P, COLS], F32, name="a")
+        b = keep.tile([P, COLS], F32, name="b")
+        c0 = keep.tile([P, COLS], F32, name="c0")
+        d0 = keep.tile([P, COLS], F32, name="d0")
+        half = SLOTS // 2
+        lo, hi = slice(0, half), slice(half, SLOTS)
+        lo_cols, hi_cols = slice(0, half // 16), slice(half // 16, SLOTS // 16)
+
+        nc.scalar.copy(a[:, :BANK], banks[("keys", 0)][:])
+        nc.vector.tensor_copy(a[:, BANK:], banks[("keys", 1)][:])
+        neg_a = keep.tile([P, SLOTS], F32, name="neg_a")
+        nc.scalar.activation(neg_a[:], a[:].indirect(tok[:]), COPY, scale=-1.0)
+        nc.vector.tensor_copy(b[:, :BANK], banks[("notes", 0)][:])
+        nc.vector.tensor_copy(b[:, BANK:], banks[("notes", 1)][:])
+        got_b = keep.tile([P, SLOTS], F32, name="got_b")
+        nc.vector.tensor_copy(got_b[:, lo], b[:].indirect(note[:, lo_cols]))
+        nc.scalar.activation(got_b[:, hi], b[:].indirect(note[:, hi_cols]), COPY)
+        for part, cols in ((lo, lo_cols), (hi, hi_cols)):
+            nc.vector.tensor_tensor(f2[:].indirect(user[:, cols]), got_b[:, part], neg_a[:, part], ADD)
+
+        nc.scalar.copy(c0[:, :BANK], banks[("users", 0)][:])
+        nc.scalar.copy(c0[:, BANK:], banks[("users", 1)][:])
+        nc.scalar.copy(d0[:, :BANK], banks[("shelves", 0)][:])
+        nc.scalar.copy(d0[:, BANK:], banks[("shelves", 1)][:])
+        neg_c = keep.tile([P, SLOTS], F32, name="neg_c")
+        got_d = keep.tile([P, SLOTS], F32, name="got_d")
+        for part, cols in ((lo, lo_cols), (hi, hi_cols)):
+            nc.scalar.activation(neg_c[:, part], c0[:].indirect(user[:, cols]), COPY, scale=-1.0)
+            nc.scalar.activation(got_d[:, part], d0[:].indirect(shelf[:, cols]), COPY)
+
+        cc = keep.tile([P, COLS], F32, name="cc")
+        nc.vector.tensor_tensor(cc[:], c0[:], f2[:], ADD)
+        for part, cols in ((lo, lo_cols), (hi, hi_cols)):
+            nc.vector.tensor_tensor(f1[:].indirect(tok[:, cols]), got_d[:, part], neg_c[:, part], ADD)
+        got_cc = keep.tile([P, SLOTS], F32, name="got_cc")
+        nc.scalar.activation(got_cc[:], cc[:].indirect(user_out[:]), COPY)
+
+        aa = keep.tile([P, COLS], F32, name="aa")
+        nc.vector.tensor_tensor(aa[:], a[:], f1[:], ADD)
+        y = keep.tile([P, SLOTS], F32, name="y")
+        got_aa = keep.tile([P, half], F32, name="got_aa")
+        nc.vector.tensor_tensor(y[:, lo], aa[:].indirect(tok_out[:, lo_cols]), got_cc[:, lo], SUBTRACT)
+        nc.sync.dma_start(out[:, lo], y[:, lo])
+        nc.scalar.activation(got_aa[:], aa[:].indirect(tok_out[:, hi_cols]), COPY)
+        nc.vector.tensor_tensor(y[:, hi], got_aa[:], got_cc[:, hi], SUBTRACT)
+        nc.sync.dma_start(out[:, hi], y[:, hi])

@@ -47,13 +47,11 @@ def tile_attend_crossgaps_four_kernel(
             "shelves": shelves_words[0].rearrange("p n t -> p (n t)"),
         }
         scales_hbm = {"keys": keys_scales, "notes": notes_scales, "users": users_scales, "shelves": shelves_scales}
-        f1 = keep.tile([P, COLS], F32, name="f1")
         f2 = keep.tile([P, COLS], F32, name="f2")
 
         for n in names:
             nc.vector.memset(planes[n][:].bitcast(I32), 0)
         nc.vector.memset(f2[:], 0.0)
-        nc.vector.memset(f1[:], 0.0)
 
         def load_scales(n):
             for quad in range(4):
@@ -87,7 +85,7 @@ def tile_attend_crossgaps_four_kernel(
         user_out = load_list(offs6, "user_out")
         tok_out = load_list(offs5, "tok_out")
 
-        q_bf = keep.tile([P, ROWS, PACK], BF16, name="q_bf", align_bytes=64)
+        q_bf = keep.tile([P, ROWS, PACK], BF16, name="q_bf", tag="q_bf_then_f1", align_bytes=64)
         nc.vector.tensor_copy(
             q_bf[:].rearrange("p (c i) t -> p c t i", i=4), q_raw[:].rearrange("p t (c i) -> p c t i", i=4)
         )
@@ -96,6 +94,9 @@ def tile_attend_crossgaps_four_kernel(
         nc.vector.quantize_mx(
             out=q_codes[:].bitcast(FP8X4), scales=q_plane[:], in_=q_bf[:].rearrange("p w t -> p (w t)")
         )
+
+        f1 = keep.tile([P, COLS], F32, name="f1", tag="q_bf_then_f1", align_bytes=64)
+        nc.vector.memset(f1[:], 0.0)
 
         banks = {}
 
@@ -118,7 +119,7 @@ def tile_attend_crossgaps_four_kernel(
         a = keep.tile([P, COLS], F32, name="a")
         b = keep.tile([P, COLS], F32, name="b")
         c0 = keep.tile([P, COLS], F32, name="c0")
-        d0 = keep.tile([P, COLS], F32, name="d0")
+        d0 = keep.tile([P, COLS], F32, name="d0", tag="d0_then_got_cc")
         half = SLOTS // 2
         lo, hi = slice(0, half), slice(half, SLOTS)
         lo_cols, hi_cols = slice(0, half // 16), slice(half // 16, SLOTS // 16)
@@ -149,7 +150,7 @@ def tile_attend_crossgaps_four_kernel(
         nc.vector.tensor_tensor(cc[:], c0[:], f2[:], ADD)
         for part, cols in ((lo, lo_cols), (hi, hi_cols)):
             nc.vector.tensor_tensor(f1[:].indirect(tok[:, cols]), got_d[:, part], neg_c[:, part], ADD)
-        got_cc = keep.tile([P, SLOTS], F32, name="got_cc")
+        got_cc = keep.tile([P, SLOTS], F32, name="got_cc", tag="d0_then_got_cc")
         nc.scalar.activation(got_cc[:], cc[:].indirect(user_out[:]), COPY)
 
         aa = keep.tile([P, COLS], F32, name="aa")

@@ -146,19 +146,23 @@ def tile_attend_crossgaps_four_kernel(
             nc.scalar.activation(neg_c[:, part], c0[:].indirect(user[:, cols]), COPY, scale=-1.0)
             nc.scalar.activation(got_d[:, part], d0[:].indirect(shelf[:, cols]), COPY)
 
+        split = 704
+
+        def add_gaps(total, n, scores, gaps):
+            nc.gpsimd.tensor_tensor(total[:, split:], scores[:, split:], gaps[:, split:], ADD)
+            nc.vector.tensor_tensor(total[:, :BANK], banks[(n, 0)][:], gaps[:, :BANK], ADD)
+            nc.vector.tensor_tensor(total[:, BANK:split], banks[(n, 1)][:, : split - BANK], gaps[:, BANK:split], ADD)
+
         cc = keep.tile([P, COLS], F32, name="cc")
-        nc.vector.tensor_tensor(cc[:], c0[:], f2[:], ADD)
+        add_gaps(cc, "users", c0, f2)
         for part, cols in ((lo, lo_cols), (hi, hi_cols)):
             nc.vector.tensor_tensor(f1[:].indirect(tok[:, cols]), got_d[:, part], neg_c[:, part], ADD)
         got_cc = keep.tile([P, SLOTS], F32, name="got_cc", tag="d0_then_got_cc")
         nc.scalar.activation(got_cc[:], cc[:].indirect(user_out[:]), COPY)
 
         aa = keep.tile([P, COLS], F32, name="aa")
-        nc.vector.tensor_tensor(aa[:], a[:], f1[:], ADD)
+        add_gaps(aa, "keys", a, f1)
         y = keep.tile([P, SLOTS], F32, name="y")
-        got_aa = keep.tile([P, half], F32, name="got_aa")
-        nc.vector.tensor_tensor(y[:, lo], aa[:].indirect(tok_out[:, lo_cols]), got_cc[:, lo], SUBTRACT)
-        nc.sync.dma_start(out[:, lo], y[:, lo])
-        nc.scalar.activation(got_aa[:], aa[:].indirect(tok_out[:, hi_cols]), COPY)
-        nc.vector.tensor_tensor(y[:, hi], got_aa[:], got_cc[:, hi], SUBTRACT)
-        nc.sync.dma_start(out[:, hi], y[:, hi])
+        for part, cols in ((lo, lo_cols), (hi, hi_cols)):
+            nc.vector.tensor_tensor(y[:, part], aa[:].indirect(tok_out[:, cols]), got_cc[:, part], SUBTRACT)
+            nc.sync.dma_start(out[:, part], y[:, part])

@@ -32,7 +32,7 @@ def tile_attend_crossgaps_four_kernel(
         keep = ctx.enter_context(tc.tile_pool(name="keep", bufs=1))
         psum = ctx.enter_context(tc.psum_pool(name="psum", bufs=1))
 
-        names = ("keys", "notes", "users", "shelves")
+        names = ("keys", "notes", "shelves", "users")
         planes = {n: keep.tile([P, COLS], U8, name=n + "_plane", align_bytes=64) for n in names}
         words = {
             "keys": keep.tile([P, 2 * COLS], U8, name="keys_codes", align_bytes=64),
@@ -50,7 +50,7 @@ def tile_attend_crossgaps_four_kernel(
         f2 = keep.tile([P, COLS], F32, name="f2")
 
         for n in names:
-            nc.vector.memset(planes[n][:].bitcast(I32), 0)
+            nc.gpsimd.memset(planes[n][:].bitcast(I32), 0)
         nc.vector.memset(f2[:], 0.0)
 
         def load_scales(n):
@@ -75,20 +75,23 @@ def tile_attend_crossgaps_four_kernel(
         load_words("notes")
         load_scales("notes")
         tok = load_list(offs, "tok")
-        load_words("users")
+        load_words("shelves")
         note = load_list(offs2, "note")
         user = load_list(offs3, "user")
-        load_scales("users")
-        load_words("shelves")
         load_scales("shelves")
+        load_words("users")
+        load_scales("users")
         shelf = load_list(offs4, "shelf")
         user_out = load_list(offs6, "user_out")
         tok_out = load_list(offs5, "tok_out")
 
         q_bf = keep.tile([P, ROWS, PACK], BF16, name="q_bf", tag="q_bf_then_f1", align_bytes=64)
-        nc.vector.tensor_copy(
-            q_bf[:].rearrange("p (c i) t -> p c t i", i=4), q_raw[:].rearrange("p t (c i) -> p c t i", i=4)
-        )
+        cast_split = 88
+        for copy, rows in ((nc.vector.tensor_copy, slice(0, cast_split)), (nc.scalar.copy, slice(cast_split, ROWS))):
+            copy(
+                q_bf[:, rows, :].rearrange("p (c i) t -> p c t i", i=4),
+                q_raw[:, :, rows].rearrange("p t (c i) -> p c t i", i=4),
+            )
         q_codes = keep.tile([P, ROWS], U32, name="q_codes", align_bytes=64)
         q_plane = keep.tile([P, ROWS], U8, name="q_plane", align_bytes=64)
         nc.vector.quantize_mx(
@@ -124,8 +127,8 @@ def tile_attend_crossgaps_four_kernel(
         lo, hi = slice(0, half), slice(half, SLOTS)
         lo_cols, hi_cols = slice(0, half // 16), slice(half // 16, SLOTS // 16)
 
-        nc.scalar.copy(a[:, :BANK], banks[("keys", 0)][:])
-        nc.vector.tensor_copy(a[:, BANK:], banks[("keys", 1)][:])
+        nc.vector.tensor_copy(a[:, :BANK], banks[("keys", 0)][:])
+        nc.scalar.copy(a[:, BANK:], banks[("keys", 1)][:])
         neg_a = keep.tile([P, SLOTS], F32, name="neg_a")
         nc.scalar.activation(neg_a[:], a[:].indirect(tok[:]), COPY, scale=-1.0)
         nc.vector.tensor_copy(b[:, :BANK], banks[("notes", 0)][:])
@@ -133,13 +136,12 @@ def tile_attend_crossgaps_four_kernel(
         got_b = keep.tile([P, SLOTS], F32, name="got_b")
         nc.vector.tensor_copy(got_b[:, lo], b[:].indirect(note[:, lo_cols]))
         nc.scalar.activation(got_b[:, hi], b[:].indirect(note[:, hi_cols]), COPY)
-        for part, cols in ((lo, lo_cols), (hi, hi_cols)):
-            nc.vector.tensor_tensor(f2[:].indirect(user[:, cols]), got_b[:, part], neg_a[:, part], ADD)
+        nc.vector.tensor_tensor(f2[:].indirect(user[:]), got_b[:], neg_a[:], ADD)
 
-        nc.scalar.copy(c0[:, :BANK], banks[("users", 0)][:])
-        nc.scalar.copy(c0[:, BANK:], banks[("users", 1)][:])
         nc.scalar.copy(d0[:, :BANK], banks[("shelves", 0)][:])
         nc.scalar.copy(d0[:, BANK:], banks[("shelves", 1)][:])
+        nc.scalar.copy(c0[:, :BANK], banks[("users", 0)][:])
+        nc.scalar.copy(c0[:, BANK:], banks[("users", 1)][:])
         neg_c = keep.tile([P, SLOTS], F32, name="neg_c")
         got_d = keep.tile([P, SLOTS], F32, name="got_d")
         for part, cols in ((lo, lo_cols), (hi, hi_cols)):

from contextlib import ExitStack

import concourse.mybir as mybir

F32 = mybir.dt.float32
BF16 = mybir.dt.bfloat16
I32 = mybir.dt.int32
U32 = mybir.dt.uint32
U16 = mybir.dt.uint16
U8 = mybir.dt.uint8
FP8X4 = mybir.dt.float8_e4m3fn_x4
FP4X4 = mybir.dt.float4_e2m1fn_x4
ADD = mybir.AluOpType.add
SUBTRACT = mybir.AluOpType.subtract
COPY = mybir.ActivationFunctionType.Copy

P = 128
PACK = 4
ROWS = 128
COLS = 1024
BANK = 512
SLOTS = 512
FLOPS = 2 * 512 * 128 * 4 * 1024


def tile_attend_crossgaps_four_kernel(
    tc, query, keys_words, keys_scales, notes_words, notes_scales, users_words, users_scales,
    shelves_words, shelves_scales, offs, offs2, offs3, offs4, offs5, offs6, out,
):
    nc = tc.nc
    with ExitStack() as ctx:
        keep = ctx.enter_context(tc.tile_pool(name="keep", bufs=1))
        psum = ctx.enter_context(tc.psum_pool(name="psum", bufs=1))

        names = ("keys", "notes", "shelves", "users")
        planes = {n: keep.tile([P, COLS], U8, name=n + "_plane", align_bytes=64) for n in names}
        words = {
            "keys": keep.tile([P, 2 * COLS], U8, name="keys_codes", align_bytes=64),
            "notes": keep.tile([P, COLS], U32, name="notes_codes", align_bytes=64),
            "users": keep.tile([P, 2 * COLS], U8, name="users_codes", align_bytes=64),
            "shelves": keep.tile([P, COLS], U32, name="shelves_codes", align_bytes=64),
        }
        words_hbm = {
            "keys": keys_words[0],
            "notes": notes_words[0].rearrange("p n t -> p (n t)"),
            "users": users_words[0],
            "shelves": shelves_words[0].rearrange("p n t -> p (n t)"),
        }
        scales_hbm = {"keys": keys_scales, "notes": notes_scales, "users": users_scales, "shelves": shelves_scales}
        f2 = keep.tile([P, COLS], F32, name="f2")

        for n in names:
            nc.gpsimd.memset(planes[n][:].bitcast(I32), 0)
        nc.vector.memset(f2[:], 0.0)

        def load_scales(n):
            for quad in range(4):
                nc.sync.dma_start(
                    planes[n][32 * quad : 32 * quad + 4, :].bitcast(I32),
                    scales_hbm[n][0, 4 * quad : 4 * quad + 4, :].bitcast(I32),
                )

        def load_words(n):
            nc.sync.dma_start(words[n][:].bitcast(I32), words_hbm[n].bitcast(I32))

        def load_list(src, name):
            t = keep.tile([P, SLOTS // 16], U16, name=name)
            nc.sync.dma_start(t[:], src)
            return t

        q_raw = keep.tile([P, PACK, ROWS], F32, name="q_raw")
        nc.sync.dma_start(q_raw[:], query.rearrange("(p j) w -> p j w", j=PACK))
        load_scales("keys")
        load_words("keys")
        load_words("notes")
        load_scales("notes")
        tok = load_list(offs, "tok")
        load_words("shelves")
        note = load_list(offs2, "note")
        user = load_list(offs3, "user")
        load_scales("shelves")
        load_words("users")
        load_scales("users")
        shelf = load_list(offs4, "shelf")
        user_out = load_list(offs6, "user_out")
        tok_out = load_list(offs5, "tok_out")

        q_bf = keep.tile([P, ROWS, PACK], BF16, name="q_bf", tag="q_bf_then_f1", align_bytes=64)
        cast_split = 88
        for copy, rows in ((nc.vector.tensor_copy, slice(0, cast_split)), (nc.scalar.copy, slice(cast_split, ROWS))):
            copy(
                q_bf[:, rows, :].rearrange("p (c i) t -> p c t i", i=4),
                q_raw[:, :, rows].rearrange("p t (c i) -> p c t i", i=4),
            )
        q_codes = keep.tile([P, ROWS], U32, name="q_codes", align_bytes=64)
        q_plane = keep.tile([P, ROWS], U8, name="q_plane", align_bytes=64)
        nc.vector.quantize_mx(
            out=q_codes[:].bitcast(FP8X4), scales=q_plane[:], in_=q_bf[:].rearrange("p w t -> p (w t)")
        )

        f1 = keep.tile([P, COLS], F32, name="f1", tag="q_bf_then_f1", align_bytes=64)
        nc.vector.memset(f1[:], 0.0)

        banks = {}

        def score(n):
            for h in range(2):
                bank = psum.tile([P, BANK], F32, name="bank_%s_%d" % (n, h))
                if n in ("keys", "users"):
                    rhs = words[n][:, 2 * BANK * h : 2 * BANK * (h + 1)].bitcast(FP4X4)
                else:
                    rhs = words[n][:, BANK * h : BANK * (h + 1)].bitcast(FP8X4)
                nc.tensor.matmul_mx(
                    out=bank[:], lhsT=q_codes[:].bitcast(FP8X4), lhsT_scale=q_plane[:],
                    rhs=rhs, rhs_scale=planes[n][:, BANK * h : BANK * (h + 1)], start=True, stop=True,
                )
                banks[(n, h)] = bank

        for n in names:
            score(n)

        a = keep.tile([P, COLS], F32, name="a")
        b = keep.tile([P, COLS], F32, name="b")
        c0 = keep.tile([P, COLS], F32, name="c0")
        d0 = keep.tile([P, COLS], F32, name="d0", tag="d0_then_got_cc")
        half = SLOTS // 2
        lo, hi = slice(0, half), slice(half, SLOTS)
        lo_cols, hi_cols = slice(0, half // 16), slice(half // 16, SLOTS // 16)

        nc.vector.tensor_copy(a[:, :BANK], banks[("keys", 0)][:])
        nc.scalar.copy(a[:, BANK:], banks[("keys", 1)][:])
        neg_a = keep.tile([P, SLOTS], F32, name="neg_a")
        nc.scalar.activation(neg_a[:], a[:].indirect(tok[:]), COPY, scale=-1.0)
        nc.vector.tensor_copy(b[:, :BANK], banks[("notes", 0)][:])
        nc.vector.tensor_copy(b[:, BANK:], banks[("notes", 1)][:])
        got_b = keep.tile([P, SLOTS], F32, name="got_b")
        nc.vector.tensor_copy(got_b[:, lo], b[:].indirect(note[:, lo_cols]))
        nc.scalar.activation(got_b[:, hi], b[:].indirect(note[:, hi_cols]), COPY)
        nc.vector.tensor_tensor(f2[:].indirect(user[:]), got_b[:], neg_a[:], ADD)

        nc.scalar.copy(d0[:, :BANK], banks[("shelves", 0)][:])
        nc.scalar.copy(d0[:, BANK:], banks[("shelves", 1)][:])
        nc.scalar.copy(c0[:, :BANK], banks[("users", 0)][:])
        nc.scalar.copy(c0[:, BANK:], banks[("users", 1)][:])
        neg_c = keep.tile([P, SLOTS], F32, name="neg_c")
        got_d = keep.tile([P, SLOTS], F32, name="got_d")
        for part, cols in ((lo, lo_cols), (hi, hi_cols)):
            nc.scalar.activation(neg_c[:, part], c0[:].indirect(user[:, cols]), COPY, scale=-1.0)
            nc.scalar.activation(got_d[:, part], d0[:].indirect(shelf[:, cols]), COPY)

        split = 704

        def add_gaps(total, n, scores, gaps):
            nc.gpsimd.tensor_tensor(total[:, split:], scores[:, split:], gaps[:, split:], ADD)
            nc.vector.tensor_tensor(total[:, :BANK], banks[(n, 0)][:], gaps[:, :BANK], ADD)
            nc.vector.tensor_tensor(total[:, BANK:split], banks[(n, 1)][:, : split - BANK], gaps[:, BANK:split], ADD)

        cc = keep.tile([P, COLS], F32, name="cc")
        add_gaps(cc, "users", c0, f2)
        for part, cols in ((lo, lo_cols), (hi, hi_cols)):
            nc.vector.tensor_tensor(f1[:].indirect(tok[:, cols]), got_d[:, part], neg_c[:, part], ADD)
        got_cc = keep.tile([P, SLOTS], F32, name="got_cc", tag="d0_then_got_cc")
        nc.scalar.activation(got_cc[:], cc[:].indirect(user_out[:]), COPY)

        aa = keep.tile([P, COLS], F32, name="aa")
        add_gaps(aa, "keys", a, f1)
        y = keep.tile([P, SLOTS], F32, name="y")
        for part, cols in ((lo, lo_cols), (hi, hi_cols)):
            nc.vector.tensor_tensor(y[:, part], aa[:].indirect(tok_out[:, cols]), got_cc[:, part], SUBTRACT)
            nc.sync.dma_start(out[:, part], y[:, part])
